import numpy as np
import ml_dtypes


def mxq(x, axis, fmt="e4m3"):
    dtype, down = {"e4m3": (ml_dtypes.float8_e4m3fn, 7), "e5m2": (ml_dtypes.float8_e5m2, 14)}[fmt]
    v = np.moveaxis(np.asarray(x, np.float32).astype(ml_dtypes.bfloat16).astype(np.float64), axis, -1)
    blocks = v.reshape(v.shape[:-1] + (-1, 32))
    amax = np.abs(blocks).max(-1, keepdims=True)
    byte = np.maximum(np.where(amax > 0, np.frexp(amax)[1] - 1 + 127, 0) - down, 1)
    scale = np.exp2(byte - 127.0)
    codes = (blocks / scale).astype(np.float32).astype(dtype).astype(np.float64)
    return np.moveaxis((codes * scale).reshape(v.shape), -1, axis)


WIDE = False


def mx_kscale(k):
    if not WIDE:
        return np.ones(k)
    levels = np.array([10, -10, 5, -5, 0])
    if k % 512:
        return np.exp2(np.random.permutation(np.resize(levels, k // 32))).repeat(32)
    a = np.empty((k // 512, 16))
    for p in range(k // 512):
        a[p, :8] = np.random.permutation(np.resize(levels, 8))
        for g in range(8):
            far = levels[np.abs(levels - a[p, g]) >= 10]
            a[p, g + 8] = far[np.random.randint(len(far))]
    return np.exp2(a.ravel()).repeat(32)


def f64(x):
    return np.asarray(x).astype(np.float64)


def striped(idx):
    return np.tile(idx.reshape(-1, 16).T, (8, 1)).astype(np.uint16)


def unstriped(offs):
    return offs[:16].T.reshape(-1).astype(np.int64)


def pack_weight(w):
    k, n = w.shape
    w = f64(np.asarray(w, np.float32).astype(ml_dtypes.bfloat16)).reshape(k // 32, 32, n)
    amax = np.abs(w).max(1)
    byte = np.clip(np.where(amax > 0, np.frexp(amax)[1] - 1 + 127 - 7, 1), 1, 254)
    scaled = (w * np.exp2(127.0 - byte)[:, None, :]).reshape(k, n).astype(np.float32)
    words = np.ascontiguousarray(scaled.reshape(k // 512, 128, 4, n).transpose(0, 1, 3, 2)).astype(ml_dtypes.float8_e4m3fn).view(np.uint8)
    return words, np.ascontiguousarray(byte.astype(np.uint8).reshape(k // 512, 16, n))


def unpack_weight(words, scales):
    g, p, n, _ = words.shape
    vals = np.ascontiguousarray(words).view(ml_dtypes.float8_e4m3fn).astype(np.float64) * np.repeat(np.exp2(scales.astype(np.float64) - 127.0), 8, axis=1)[..., None]
    return vals.transpose(0, 1, 3, 2).reshape(g * 512, n)


E2M1 = np.array([0.0, 0.5, 1.0, 1.5, 2.0, 3.0, 4.0, 6.0, -0.0, -0.5, -1.0, -1.5, -2.0, -3.0, -4.0, -6.0])


def pack_fp4(w):
    k, n = w.shape
    w = f64(np.asarray(w, np.float32).astype(ml_dtypes.bfloat16)).reshape(k // 32, 32, n)
    amax = np.abs(w).max(1)
    mant, ex = np.frexp(amax / 6.0)
    byte = np.clip(np.where(amax > 0, np.where(mant > 0.5, ex, ex - 1) + 127, 1), 1, 254)
    scaled = (w * np.exp2(127.0 - byte)[:, None, :]).reshape(k, n).astype(np.float32)
    c = np.ascontiguousarray(scaled.reshape(k // 512, 128, 4, n).transpose(0, 1, 3, 2)).astype(ml_dtypes.float4_e2m1fn).view(np.uint8) & 0xF
    words = (c[..., 0::2] | (c[..., 1::2] << 4)).reshape(k // 512, 128, 2 * n)
    return np.ascontiguousarray(words), np.ascontiguousarray(byte.astype(np.uint8).reshape(k // 512, 16, n))


def unpack_fp4(words, scales):
    g, _, n = scales.shape
    words = np.ascontiguousarray(words).reshape(g, 128, n, 2)
    nib = np.empty((g, 128, n, 4), np.uint8)
    nib[..., 0::2] = words & 0xF
    nib[..., 1::2] = words >> 4
    vals = E2M1[nib] * np.repeat(np.exp2(scales.astype(np.float64) - 127.0), 8, axis=1)[..., None]
    return vals.transpose(0, 1, 3, 2).reshape(g * 512, n)


K, T, S, N, H = 1024, 2048, 512, 256, 512


def setup_inputs():
    n = np.random.standard_normal
    s = mx_kscale(K)[:, None]
    u = mx_kscale(H)
    packed_xT = pack_weight(n((K, T)) * s)
    packed_w1 = pack_fp4(n((K, H)) / np.sqrt(K) / s)
    packed_w2 = pack_fp4(n((H, N)) / np.sqrt(H) / u[:, None])
    return {
        "x_words": packed_xT[0],
        "x_scales": packed_xT[1],
        "w1_words": packed_w1[0],
        "w1_scales": packed_w1[1],
        "h1": (np.random.uniform(0.1, 1.5, (H, S))).astype(np.float32),
        "h2": (np.random.uniform(0.1, 1.5, (H, S))).astype(np.float32),
        "rho": (np.random.uniform(0.1, 0.8, (H, S))).astype(np.float32),
        "unit": (np.random.uniform(0.6, 1.4, (H, 1)) * u[:, None]).astype(np.float32),
        "w2_words": packed_w2[0],
        "w2_scales": packed_w2[1],
        "offs": striped(np.random.permutation(T)[:S]),
        "n1": striped(np.random.permutation(S)),
        "n2": striped(np.random.permutation(S)),
    }


def reference(x_words, x_scales, w1_words, w1_scales, h1, h2, rho, unit, w2_words, w2_scales, offs, n1, n2):
    c1 = np.exp(-1.0 * f64(h1))
    c2 = np.exp(-1.0 * f64(h2))
    dn = -1.0 * (0.9 * ((f64(rho)) ** 2)) + 1.05
    we1 = (c1 - (f64(rho) * c2)) / dn
    xq = unpack_weight(x_words, x_scales)[:, unstriped(offs)]
    y = unpack_fp4(w1_words, w1_scales).T @ xq
    y1 = y[:, unstriped(n1)]
    we2 = (c2 - (f64(rho) * c1)) / dn
    y2 = y[:, unstriped(n2)]
    kr = we1 * y1 + we2 * y2
    kvar = -1.0 * (0.9 * (we1 * c1 + we2 * c2)) + 1.0
    hid = f64(unit) * (kr * kvar)
    return unpack_fp4(w2_words, w2_scales).T @ mxq(hid, 0, "e4m3")

@@ -1,0 +1,264 @@
+import math
+from contextlib import ExitStack
+
+import concourse.mybir as mybir
+from concourse.masks import make_identity
+
+K, T, S, N, H = 1024, 2048, 512, 256, 512
+FLOPS = 2 * K * H * S + 2 * H * N * S
+
+F32 = mybir.dt.float32
+BF16 = mybir.dt.bfloat16
+I32 = mybir.dt.int32
+U32 = mybir.dt.uint32
+U16 = mybir.dt.uint16
+U8 = mybir.dt.uint8
+FP8X4 = mybir.dt.float8_e4m3fn_x4
+FP4X4 = mybir.dt.float4_e2m1fn_x4
+ALU = mybir.AluOpType
+ACT = mybir.ActivationFunctionType
+
+P = 128
+PASSES = K // 512
+TILES = H // P
+BLOCKS = S // P
+HALF = S // 2
+PAD = 1.05 / 0.9
+ROOT = math.sqrt(0.9)
+
+
+def tile_picked_yskrig_var_p_kernel(
+    tc, x_words, x_scales, w1_words, w1_scales, h1, h2, rho, unit, w2_words, w2_scales, offs, n1, n2, out
+):
+    nc = tc.nc
+    with ExitStack() as ctx:
+        keep = ctx.enter_context(tc.tile_pool(name="keep", bufs=1))
+        work = ctx.enter_context(tc.tile_pool(name="work", bufs=2))
+        psum = ctx.enter_context(tc.psum_pool(name="psum", bufs=1))
+
+        def load_scale_rows(queue, plane, scales):
+            for q in range(4):
+                queue.dma_start(
+                    out=plane[32 * q : 32 * q + 4, :, :].bitcast(I32),
+                    in_=scales[:, 4 * q : 4 * q + 4, :].rearrange("o r c -> r o c").bitcast(I32),
+                )
+
+        def load_x_plane(queues):
+            for q in range(4):
+                queues[q].dma_start(
+                    out=x_plane[32 * q : 32 * q + 4 * PASSES, :].bitcast(I32),
+                    in_=x_scales[:, 4 * q : 4 * q + 4, :].bitcast(I32),
+                )
+
+        def add_transposed(bank_cols, terms):
+            for n, term in enumerate(terms):
+                nc.tensor.matmul(
+                    bank_cols, lhsT=term, rhs=ident[:], start=(n == 0), stop=(n == len(terms) - 1), is_transpose=True
+                )
+
+        offs_sb = keep.tile([P, S // 16], U16, name="offs_sb")
+        n_sb = [keep.tile([P, S // 16], U16, name=f"n{k}_sb") for k in (1, 2)]
+        x_plane = keep.tile([P, T], U8, name="x_plane", align_bytes=64)
+        w1_plane = keep.tile([P, PASSES, H], U8, name="w1_plane", align_bytes=64)
+        w2_plane = keep.tile([P, 1, N], U8, name="w2_plane", align_bytes=64)
+        ident = keep.tile([P, P], F32, name="ident")
+        x_sb = [keep.tile([P, T], I32, name=f"x_sb{o}", align_bytes=64) for o in range(PASSES)]
+        w1_sb = keep.tile([P, PASSES, 2 * H], U8, name="w1_sb", align_bytes=64)
+        w2_sb = keep.tile([P, 2 * N], U8, name="w2_sb", align_bytes=64)
+        unit_sb = keep.tile([P, TILES], F32, name="unit_sb")
+        rho_sb = keep.tile([P, TILES, S], F32, name="rho_sb")
+        h_sb = [[keep.tile([P, S], F32, name=f"h{k}_{t}") for k in range(2)] for t in range(TILES)]
+
+        nc.vector.memset(x_plane[:].bitcast(I32), 0)
+        nc.gpsimd.memset(w1_plane[:].bitcast(I32), 0)
+        nc.gpsimd.memset(w2_plane[:].bitcast(I32), 0)
+        make_identity(nc, ident[:])
+
+        def load_h(t, queues=(nc.sync, nc.sync)):
+            for k, h in enumerate((h1, h2)):
+                queues[k].dma_start(out=h_sb[t][k][:], in_=h[P * t : P * (t + 1), :])
+
+        def load_rho(first, count, queue=nc.sync):
+            rows = rho[P * first : P * (first + count), :].rearrange("(t p) j -> p t j", p=P)
+            queue.dma_start(out=rho_sb[:, first : first + count, :], in_=rows)
+
+        def load_x(o):
+            nc.sync.dma_start(out=x_sb[o][:], in_=x_words[o].rearrange("p c r -> p (c r)").bitcast(I32))
+
+        load_h(0, (nc.sync, nc.scalar))
+        load_rho(0, 1)
+        load_rho(1, 1, nc.scalar)
+        load_rho(2, 1)
+        load_rho(3, 1, nc.scalar)
+        load_x_plane((nc.sync, nc.sync, nc.sync, nc.sync))
+        nc.sync.dma_start(offs_sb[:], offs)
+        load_x(0)
+        load_h(1)
+        load_x(1)
+        nc.sync.dma_start(out=w1_sb[:].bitcast(I32), in_=w1_words.rearrange("o p c -> p o c").bitcast(I32))
+        load_h(2)
+        load_h(3)
+        nc.sync.dma_start(n_sb[0][:], n1)
+        nc.sync.dma_start(n_sb[1][:], n2)
+        load_scale_rows(nc.sync, w2_plane, w2_scales)
+        nc.sync.dma_start(out=w2_sb[:].bitcast(I32), in_=w2_words[0].bitcast(I32))
+        load_scale_rows(nc.gpsimd, w1_plane, w1_scales)
+        with nc.allow_non_contiguous_dma(reason="one value a row"):
+            nc.gpsimd.dma_start(out=unit_sb[:], in_=unit.rearrange("(t p) o -> p (t o)", p=P))
+
+        sq = keep.tile([P, TILES, S], F32, name="sq")
+        dn2 = keep.tile([P, TILES, S], F32, name="dn2")
+        log_dn2 = keep.tile([P, TILES, S], F32, name="log_dn2")
+        cov = keep.tile([P, 2, TILES, S], F32, name="cov")
+        inv_dn2 = keep.tile([P, TILES, S], F32, name="inv_dn2")
+        a_sb = keep.tile([P, 2, TILES, S], F32, name="a_sb")
+        prod = keep.tile([P, 2, TILES, S], F32, name="prod")
+        factor = keep.tile([P, TILES, S], F32, name="factor")
+        xg_words = [keep.tile([P, S], U32, name=f"xg_words{o}", align_bytes=64) for o in range(PASSES)]
+        xg_plane = [keep.tile([P, S], U8, name=f"xg_plane{o}", align_bytes=64) for o in range(PASSES)]
+        y_bank = [psum.tile([P, S], F32, name=f"y_bank{t}", tag=f"wide{t}") for t in range(TILES)]
+        y_sb = [keep.tile([P, S], F32, name=f"y_sb{t}") for t in range(TILES)]
+
+        nc.gpsimd.memset(xg_plane[1][:].bitcast(I32), 0)
+
+        def covariances(t):
+            for k in range(2):
+                nc.scalar.activation(cov[:, k, t, :], h_sb[t][k][:], ACT.Exp, scale=-1.0)
+
+        def squares(t):
+            if t < 4:
+                nc.vector.tensor_tensor(sq[:, t, :], rho_sb[:, t, :], rho_sb[:, t, :], ALU.mult)
+            else:
+                nc.scalar.activation(sq[:, t, :], rho_sb[:, t, :], ACT.Square)
+            nc.scalar.activation(dn2[:, t, :], sq[:, t, :], ACT.Square, bias=1.05 / ROOT, scale=-ROOT)
+
+        def weights(t):
+            cross = work.tile([P, 2, S], F32, name="cross")
+            for k in (1, 0):
+                nc.vector.tensor_tensor(cross[:, k, :], rho_sb[:, t, :], cov[:, 1 - k, t, :], ALU.mult)
+            for k in (1, 0):
+                nc.vector.tensor_tensor(a_sb[:, k, t, :], cross[:, k, :], cov[:, k, t, :], ALU.subtract)
+            for k in (1, 0):
+                nc.vector.scalar_tensor_tensor(
+                    prod[:, k, t, :], a_sb[:, k, t, :], -1.0, cov[:, k, t, :], ALU.mult, ALU.mult
+                )
+
+        def first_product(o):
+            nc.vector.tensor_copy(xg_words[o][:], x_sb[o][:].bitcast(U32).indirect(offs_sb[:]))
+            for t in range(TILES):
+                nc.tensor.matmul_mx(
+                    out=y_bank[t][:],
+                    lhsT=w1_sb[:, o, 2 * P * t : 2 * P * (t + 1)].bitcast(FP4X4),
+                    lhsT_scale=w1_plane[:, o, P * t : P * (t + 1)],
+                    rhs=xg_words[o][:].bitcast(FP8X4),
+                    rhs_scale=xg_plane[o][:],
+                    start=(o == 0),
+                    stop=(o == PASSES - 1),
+                )
+
+        def gather_planes(queue):
+            nc.vector.tensor_copy(xg_plane[0][:], x_plane[:].indirect(offs_sb[:]))
+            for q in range(4):
+                queue.dma_start(
+                    out=xg_plane[1][32 * q : 32 * q + 4, :].bitcast(I32),
+                    in_=xg_plane[0][32 * q + 4 : 32 * q + 8, :].bitcast(I32),
+                )
+
+        def inverse(t):
+            log_bank = psum.tile([P, S], F32, name="log_bank", tag="turn", bufs=2)
+            for b in range(BLOCKS):
+                add_transposed(log_bank[:, P * b : P * (b + 1)], [log_dn2[:, t, P * b : P * (b + 1)]])
+            nc.scalar.activation(inv_dn2[:, t, :], log_bank[:], ACT.Exp, scale=-1.0)
+
+        def variance(t):
+            var_bank = psum.tile([P, S], F32, name="var_bank", tag="late", bufs=2)
+            for b in range(BLOCKS):
+                cols = slice(P * b, P * (b + 1))
+                add_transposed(var_bank[:, cols], [prod[:, 1, t, cols], prod[:, 0, t, cols], sq[:, t, cols]])
+            nc.vector.scalar_tensor_tensor(factor[:, t, :], var_bank[:], -PAD, inv_dn2[:, t, :], ALU.add, ALU.mult)
+
+        def leave_bank(t):
+            if t < 0:
+                nc.vector.tensor_scalar(y_sb[t][:], y_bank[t][:], unit_sb[:, t : t + 1], None, ALU.mult)
+            else:
+                nc.scalar.activation(y_sb[t][:], y_bank[t][:], ACT.Copy, scale=unit_sb[:, t : t + 1])
+
+        def neighbours(first, count, t):
+            width = P * count
+            cols = slice(P * first, P * first + width)
+            entries = slice(P // 16 * first, P // 16 * (first + count))
+            picked = work.tile([P, 2, width], F32, name="picked", bufs=8)
+            term = work.tile([P, 2, width], F32, name="term", bufs=3)
+            for k in range(2):
+                nc.scalar.activation(picked[:, k, :], y_sb[t][:].indirect(n_sb[k][:, entries]), ACT.Copy)
+            nc.vector.tensor_tensor(term[:], picked[:], a_sb[:, :, t, cols], ALU.mult)
+            for bb in range(count):
+                part = slice(P * bb, P * (bb + 1))
+                add_transposed(sum_bank[first + bb][:, t, :], [term[:, 0, part], term[:, 1, part]])
+
+        def second_product(first, count, copy_words, copy_result):
+            width = P * count
+            word_bank = psum.tile([P, count, 2, P], F32, name="word_bank", tag="turn", bufs=2)
+            for bb in range(count):
+                b = first + bb
+                hid = work.tile([P, H], BF16, name="hid", bufs=4)
+                nc.vector.tensor_tensor(
+                    hid[:].rearrange("j (t p) -> j t p", p=P), sum_bank[b][:], factor[:, :, P * b : P * (b + 1)], ALU.mult
+                )
+                words = hid[:].bitcast(F32)
+                for u in range(2):
+                    nc.tensor.transpose(word_bank[:, bb, u, :], words[:, u : H // 2 : 2], ident[:])
+            grouped = work.tile([P, width * 4], BF16, name="grouped", align_bytes=64, bufs=3)
+            copy_words(
+                grouped[:].bitcast(F32).rearrange("p (b j u) -> p b j u", b=count, u=2),
+                word_bank[:].rearrange("p b u j -> p b j u"),
+            )
+            codes = work.tile([P, width], U32, name="codes", align_bytes=64, bufs=3)
+            plane = work.tile([P, width], U8, name="plane", align_bytes=64, bufs=3)
+            nc.vector.quantize_mx(out=codes[:].bitcast(FP8X4), scales=plane[:], in_=grouped[:])
+            out_bank = psum.tile([P, 2, width], F32, name="out_bank", tag="late", bufs=2)
+            for m in range(2):
+                nc.tensor.matmul_mx(
+                    out=out_bank[:, m, :],
+                    lhsT=w2_sb[:, 2 * P * m : 2 * P * (m + 1)].bitcast(FP4X4),
+                    lhsT_scale=w2_plane[:, 0, P * m : P * (m + 1)],
+                    rhs=codes[:].bitcast(FP8X4),
+                    rhs_scale=plane[:],
+                    start=True,
+                    stop=True,
+                )
+            result = work.tile([P, 2, width], F32, name="result", bufs=3)
+            copy_result(result[:], out_bank[:])
+            nc.sync.dma_start(
+                out=out.rearrange("(m p) j -> p m j", p=P)[:, :, P * first : P * first + width], in_=result[:]
+            )
+
+        covariances(0)
+        for t in range(TILES):
+            squares(t)
+        nc.scalar.activation(log_dn2[:], dn2[:], ACT.Ln)
+        gather_planes(nc.gpsimd)
+        first_product(0)
+        first_product(1)
+        weights(0)
+        covariances(1)
+        covariances(2)
+        inverse(0)
+        weights(1)
+        variance(0)
+        covariances(3)
+        for t in range(TILES):
+            leave_bank(t)
+        sum_bank = [psum.tile([P, TILES, P], F32, name=f"sum_bank{b}", tag=f"wide{b}") for b in range(BLOCKS)]
+        for t in range(1, TILES):
+            inverse(t)
+        weights(2)
+        variance(1)
+        weights(3)
+        variance(2)
+        variance(3)
+        for first, count in ((0, 2), (2, 2)):
+            for t in range(TILES):
+                neighbours(first, count, t)
+        for first, count in ((0, 2), (2, 1), (3, 1)):
+            second_product(first, count, nc.scalar.copy, nc.scalar.copy)

@@ -50,11 +50,8 @@ def tile_picked_yskrig_var_p_kernel(
                     in_=x_scales[:, 4 * q : 4 * q + 4, :].bitcast(I32),
                 )
 
-        def add_transposed(bank_cols, terms):
-            for n, term in enumerate(terms):
-                nc.tensor.matmul(
-                    bank_cols, lhsT=term, rhs=ident[:], start=(n == 0), stop=(n == len(terms) - 1), is_transpose=True
-                )
+        def add_transposed(bank_cols, term, start, stop):
+            nc.tensor.matmul(bank_cols, lhsT=term, rhs=ident[:], start=start, stop=stop, is_transpose=True)
 
         offs_sb = keep.tile([P, S // 16], U16, name="offs_sb")
         n_sb = [keep.tile([P, S // 16], U16, name=f"n{k}_sb") for k in (1, 2)]
@@ -69,6 +66,8 @@ def tile_picked_yskrig_var_p_kernel(
         rho_sb = keep.tile([P, TILES, S], F32, name="rho_sb")
         h_sb = [[keep.tile([P, S], F32, name=f"h{k}_{t}") for k in range(2)] for t in range(TILES)]
 
+        xg_words = [keep.tile([P, S], U32, name=f"xg_words{o}", align_bytes=64) for o in range(PASSES)]
+        xg_plane = [keep.tile([P, S], U8, name=f"xg_plane{o}", align_bytes=64) for o in range(PASSES)]
         nc.vector.memset(x_plane[:].bitcast(I32), 0)
         nc.gpsimd.memset(w1_plane[:].bitcast(I32), 0)
         nc.gpsimd.memset(w2_plane[:].bitcast(I32), 0)
@@ -85,15 +84,13 @@ def tile_picked_yskrig_var_p_kernel(
         def load_x(o):
             nc.sync.dma_start(out=x_sb[o][:], in_=x_words[o].rearrange("p c r -> p (c r)").bitcast(I32))
 
-        load_h(0, (nc.sync, nc.scalar))
-        load_rho(0, 1)
-        load_rho(1, 1, nc.scalar)
-        load_rho(2, 1)
-        load_rho(3, 1, nc.scalar)
-        load_x_plane((nc.sync, nc.sync, nc.sync, nc.sync))
+        load_x_plane((nc.scalar, nc.scalar, nc.scalar, nc.gpsimd))
+        for t in range(TILES):
+            load_rho(t, 1)
+        load_h(0)
         nc.sync.dma_start(offs_sb[:], offs)
-        load_x(0)
         load_h(1)
+        load_x(0)
         load_x(1)
         nc.sync.dma_start(out=w1_sb[:].bitcast(I32), in_=w1_words.rearrange("o p c -> p o c").bitcast(I32))
         load_h(2)
@@ -114,23 +111,20 @@ def tile_picked_yskrig_var_p_kernel(
         a_sb = keep.tile([P, 2, TILES, S], F32, name="a_sb")
         prod = keep.tile([P, 2, TILES, S], F32, name="prod")
         factor = keep.tile([P, TILES, S], F32, name="factor")
-        xg_words = [keep.tile([P, S], U32, name=f"xg_words{o}", align_bytes=64) for o in range(PASSES)]
-        xg_plane = [keep.tile([P, S], U8, name=f"xg_plane{o}", align_bytes=64) for o in range(PASSES)]
-        y_bank = [psum.tile([P, S], F32, name=f"y_bank{t}", tag=f"wide{t}") for t in range(TILES)]
+        var_bank = [psum.tile([P, S], F32, name=f"var_bank{t}", tag=f"var{t}") for t in range(TILES)]
         y_sb = [keep.tile([P, S], F32, name=f"y_sb{t}") for t in range(TILES)]
-
-        nc.gpsimd.memset(xg_plane[1][:].bitcast(I32), 0)
 
         def covariances(t):
             for k in range(2):
                 nc.scalar.activation(cov[:, k, t, :], h_sb[t][k][:], ACT.Exp, scale=-1.0)
 
         def squares(t):
-            if t < 4:
-                nc.vector.tensor_tensor(sq[:, t, :], rho_sb[:, t, :], rho_sb[:, t, :], ALU.mult)
-            else:
-                nc.scalar.activation(sq[:, t, :], rho_sb[:, t, :], ACT.Square)
-            nc.scalar.activation(dn2[:, t, :], sq[:, t, :], ACT.Square, bias=1.05 / ROOT, scale=-ROOT)
+            nc.vector.tensor_tensor(sq[:, t, :], rho_sb[:, t, :], rho_sb[:, t, :], ALU.mult)
+            sq_bank = psum.tile([P, S], F32, name="sq_bank", tag=f"wide{t}")
+            for b in range(BLOCKS):
+                cols = slice(P * b, P * (b + 1))
+                add_transposed(sq_bank[:, cols], sq[:, t, cols], True, True)
+            nc.scalar.activation(dn2[:, t, :], sq_bank[:], ACT.Square, bias=1.05 / ROOT, scale=-ROOT)
 
         def weights(t):
             cross = work.tile([P, 2, S], F32, name="cross")
@@ -143,8 +137,10 @@ def tile_picked_yskrig_var_p_kernel(
                     prod[:, k, t, :], a_sb[:, k, t, :], -1.0, cov[:, k, t, :], ALU.mult, ALU.mult
                 )
 
-        def first_product(o):
+        def gather_words(o):
             nc.vector.tensor_copy(xg_words[o][:], x_sb[o][:].bitcast(U32).indirect(offs_sb[:]))
+
+        def first_product(o):
             for t in range(TILES):
                 nc.tensor.matmul_mx(
                     out=y_bank[t][:],
@@ -156,8 +152,13 @@ def tile_picked_yskrig_var_p_kernel(
                     stop=(o == PASSES - 1),
                 )
 
-        def gather_planes(queue):
+        def leave_bank(t):
+            nc.scalar.activation(y_sb[t][:], y_bank[t][:], ACT.Copy, scale=unit_sb[:, t : t + 1])
+
+        def gather_planes():
             nc.vector.tensor_copy(xg_plane[0][:], x_plane[:].indirect(offs_sb[:]))
+
+        def move_plane(queue):
             for q in range(4):
                 queue.dma_start(
                     out=xg_plane[1][32 * q : 32 * q + 4, :].bitcast(I32),
@@ -165,40 +166,35 @@ def tile_picked_yskrig_var_p_kernel(
                 )
 
         def inverse(t):
-            log_bank = psum.tile([P, S], F32, name="log_bank", tag="turn", bufs=2)
-            for b in range(BLOCKS):
-                add_transposed(log_bank[:, P * b : P * (b + 1)], [log_dn2[:, t, P * b : P * (b + 1)]])
-            nc.scalar.activation(inv_dn2[:, t, :], log_bank[:], ACT.Exp, scale=-1.0)
+            nc.scalar.activation(inv_dn2[:, t, :], log_dn2[:, t, :], ACT.Exp, scale=-1.0)
 
-        def variance(t):
-            var_bank = psum.tile([P, S], F32, name="var_bank", tag="late", bufs=2)
+        def turn_variance(t):
             for b in range(BLOCKS):
                 cols = slice(P * b, P * (b + 1))
-                add_transposed(var_bank[:, cols], [prod[:, 1, t, cols], prod[:, 0, t, cols], sq[:, t, cols]])
-            nc.vector.scalar_tensor_tensor(factor[:, t, :], var_bank[:], -PAD, inv_dn2[:, t, :], ALU.add, ALU.mult)
+                terms = (prod[:, 1, t, cols], prod[:, 0, t, cols], sq[:, t, cols])
+                for n, term in enumerate(terms):
+                    add_transposed(var_bank[t][:, cols], term, n == 0, n == len(terms) - 1)
 
-        def leave_bank(t):
-            if t < 0:
-                nc.vector.tensor_scalar(y_sb[t][:], y_bank[t][:], unit_sb[:, t : t + 1], None, ALU.mult)
-            else:
-                nc.scalar.activation(y_sb[t][:], y_bank[t][:], ACT.Copy, scale=unit_sb[:, t : t + 1])
+        def variance(t):
+            nc.vector.scalar_tensor_tensor(factor[:, t, :], var_bank[t][:], -PAD, inv_dn2[:, t, :], ALU.add, ALU.mult)
 
         def neighbours(first, count, t):
             width = P * count
             cols = slice(P * first, P * first + width)
             entries = slice(P // 16 * first, P // 16 * (first + count))
             picked = work.tile([P, 2, width], F32, name="picked", bufs=8)
-            term = work.tile([P, 2, width], F32, name="term", bufs=3)
+            term = work.tile([P, 2, width], F32, name="term", bufs=8)
             for k in range(2):
                 nc.scalar.activation(picked[:, k, :], y_sb[t][:].indirect(n_sb[k][:, entries]), ACT.Copy)
             nc.vector.tensor_tensor(term[:], picked[:], a_sb[:, :, t, cols], ALU.mult)
             for bb in range(count):
                 part = slice(P * bb, P * (bb + 1))
-                add_transposed(sum_bank[first + bb][:, t, :], [term[:, 0, part], term[:, 1, part]])
+                for k in range(2):
+                    add_transposed(sum_bank[first + bb][:, t, :], term[:, k, part], k == 0, k == 1)
 
-        def second_product(first, count, copy_words, copy_result):
+        def second_product(first, count, copy_words, copy_result, word_tag, out_tag):
             width = P * count
-            word_bank = psum.tile([P, count, 2, P], F32, name="word_bank", tag="turn", bufs=2)
+            word_bank = psum.tile([P, count, 2, P], F32, name="word_bank", tag=word_tag)
             for bb in range(count):
                 b = first + bb
                 hid = work.tile([P, H], BF16, name="hid", bufs=4)
@@ -216,7 +212,7 @@ def tile_picked_yskrig_var_p_kernel(
             codes = work.tile([P, width], U32, name="codes", align_bytes=64, bufs=3)
             plane = work.tile([P, width], U8, name="plane", align_bytes=64, bufs=3)
             nc.vector.quantize_mx(out=codes[:].bitcast(FP8X4), scales=plane[:], in_=grouped[:])
-            out_bank = psum.tile([P, 2, width], F32, name="out_bank", tag="late", bufs=2)
+            out_bank = psum.tile([P, 2, width], F32, name="out_bank", tag=out_tag)
             for m in range(2):
                 nc.tensor.matmul_mx(
                     out=out_bank[:, m, :],
@@ -236,29 +232,36 @@ def tile_picked_yskrig_var_p_kernel(
         covariances(0)
         for t in range(TILES):
             squares(t)
+        covariances(1)
         nc.scalar.activation(log_dn2[:], dn2[:], ACT.Ln)
-        gather_planes(nc.gpsimd)
+        gather_planes()
+        move_plane(nc.gpsimd)
+        gather_words(0)
+        gather_words(1)
+        y_bank = [psum.tile([P, S], F32, name=f"y_bank{t}", tag=f"wide{t}") for t in range(TILES)]
         first_product(0)
         first_product(1)
-        weights(0)
-        covariances(1)
+        for t in range(2):
+            weights(t)
+            turn_variance(t)
         covariances(2)
-        inverse(0)
-        weights(1)
-        variance(0)
         covariances(3)
         for t in range(TILES):
             leave_bank(t)
-        sum_bank = [psum.tile([P, TILES, P], F32, name=f"sum_bank{b}", tag=f"wide{b}") for b in range(BLOCKS)]
-        for t in range(1, TILES):
+        for t in range(TILES):
             inverse(t)
-        weights(2)
-        variance(1)
-        weights(3)
-        variance(2)
-        variance(3)
-        for first, count in ((0, 2), (2, 2)):
-            for t in range(TILES):
-                neighbours(first, count, t)
-        for first, count in ((0, 2), (2, 1), (3, 1)):
-            second_product(first, count, nc.scalar.copy, nc.scalar.copy)
+        sum_bank = [psum.tile([P, TILES, P], F32, name=f"sum_bank{b}", tag=f"wide{b}") for b in range(BLOCKS)]
+        for t in range(2, TILES):
+            weights(t)
+            turn_variance(t)
+        for t in range(TILES - 1):
+            variance(t)
+        for t in range(TILES - 1):
+            neighbours(0, 2, t)
+        variance(TILES - 1)
+        neighbours(0, 2, TILES - 1)
+        second_product(0, 2, nc.scalar.copy, nc.scalar.copy, "var0", "var1")
+        for t in range(TILES):
+            neighbours(2, 2, t)
+        second_product(2, 1, nc.scalar.copy, nc.scalar.copy, "var2", "wide0")
+        second_product(3, 1, nc.scalar.copy, nc.vector.tensor_copy, "var3", "wide1")

@@ -64,18 +64,15 @@ def tile_picked_yskrig_var_p_kernel(
         w2_sb = keep.tile([P, 2 * N], U8, name="w2_sb", align_bytes=64)
         unit_sb = keep.tile([P, TILES], F32, name="unit_sb")
         rho_sb = keep.tile([P, TILES, S], F32, name="rho_sb")
-        h_sb = [[keep.tile([P, S], F32, name=f"h{k}_{t}") for k in range(2)] for t in range(TILES)]
+        h_sb = [[keep.tile([P, S], F32, name=f"h{k}_{t}", tag=f"h{k}_{t}") for k in range(2)] for t in range(TILES)]
 
         xg_words = [keep.tile([P, S], U32, name=f"xg_words{o}", align_bytes=64) for o in range(PASSES)]
         xg_plane = [keep.tile([P, S], U8, name=f"xg_plane{o}", align_bytes=64) for o in range(PASSES)]
-        nc.vector.memset(x_plane[:].bitcast(I32), 0)
-        nc.gpsimd.memset(w1_plane[:].bitcast(I32), 0)
-        nc.gpsimd.memset(w2_plane[:].bitcast(I32), 0)
         make_identity(nc, ident[:])
+        nc.vector.memset(x_plane[:].bitcast(I32), 0)
 
-        def load_h(t, queues=(nc.sync, nc.sync)):
-            for k, h in enumerate((h1, h2)):
-                queues[k].dma_start(out=h_sb[t][k][:], in_=h[P * t : P * (t + 1), :])
+        def load_h(k, t, queue=nc.sync):
+            queue.dma_start(out=h_sb[t][k][:], in_=(h1, h2)[k][P * t : P * (t + 1), :])
 
         def load_rho(first, count, queue=nc.sync):
             rows = rho[P * first : P * (first + count), :].rearrange("(t p) j -> p t j", p=P)
@@ -84,34 +81,38 @@ def tile_picked_yskrig_var_p_kernel(
         def load_x(o):
             nc.sync.dma_start(out=x_sb[o][:], in_=x_words[o].rearrange("p c r -> p (c r)").bitcast(I32))
 
-        load_x_plane((nc.scalar, nc.scalar, nc.scalar, nc.gpsimd))
-        for t in range(TILES):
-            load_rho(t, 1)
-        load_h(0)
+        load_rho(0, 1)
+        load_rho(1, 1)
+        load_rho(2, 1)
+        load_rho(3, 1)
+        load_h(0, 0)
+        load_h(1, 0)
+        load_h(0, 1)
+        load_h(1, 1)
+        load_x_plane((nc.sync,) * 4)
         nc.sync.dma_start(offs_sb[:], offs)
-        load_h(1)
         load_x(0)
+        load_h(0, 2)
+        load_h(1, 2)
         load_x(1)
         nc.sync.dma_start(out=w1_sb[:].bitcast(I32), in_=w1_words.rearrange("o p c -> p o c").bitcast(I32))
-        load_h(2)
-        load_h(3)
+        load_h(0, 3)
+        load_h(1, 3)
+        load_scale_rows(nc.sync, w1_plane, w1_scales)
+        with nc.allow_non_contiguous_dma(reason="one value a row"):
+            nc.sync.dma_start(out=unit_sb[:], in_=unit.rearrange("(t p) o -> p (t o)", p=P))
         nc.sync.dma_start(n_sb[0][:], n1)
         nc.sync.dma_start(n_sb[1][:], n2)
-        load_scale_rows(nc.sync, w2_plane, w2_scales)
-        nc.sync.dma_start(out=w2_sb[:].bitcast(I32), in_=w2_words[0].bitcast(I32))
-        load_scale_rows(nc.gpsimd, w1_plane, w1_scales)
-        with nc.allow_non_contiguous_dma(reason="one value a row"):
-            nc.gpsimd.dma_start(out=unit_sb[:], in_=unit.rearrange("(t p) o -> p (t o)", p=P))
+
 
         sq = keep.tile([P, TILES, S], F32, name="sq")
         dn2 = keep.tile([P, TILES, S], F32, name="dn2")
         log_dn2 = keep.tile([P, TILES, S], F32, name="log_dn2")
         cov = keep.tile([P, 2, TILES, S], F32, name="cov")
-        inv_dn2 = keep.tile([P, TILES, S], F32, name="inv_dn2")
         a_sb = keep.tile([P, 2, TILES, S], F32, name="a_sb")
         prod = keep.tile([P, 2, TILES, S], F32, name="prod")
         factor = keep.tile([P, TILES, S], F32, name="factor")
-        var_bank = [psum.tile([P, S], F32, name=f"var_bank{t}", tag=f"var{t}") for t in range(TILES)]
+        var_bank = {}
         y_sb = [keep.tile([P, S], F32, name=f"y_sb{t}") for t in range(TILES)]
 
         def covariances(t):
@@ -168,7 +169,8 @@ def tile_picked_yskrig_var_p_kernel(
         def inverse(t):
             nc.scalar.activation(inv_dn2[:, t, :], log_dn2[:, t, :], ACT.Exp, scale=-1.0)
 
-        def turn_variance(t):
+        def turn_variance(t, tag):
+            var_bank[t] = psum.tile([P, S], F32, name="var_bank", tag=tag)
             for b in range(BLOCKS):
                 cols = slice(P * b, P * (b + 1))
                 terms = (prod[:, 1, t, cols], prod[:, 0, t, cols], sq[:, t, cols])
@@ -183,7 +185,7 @@ def tile_picked_yskrig_var_p_kernel(
             cols = slice(P * first, P * first + width)
             entries = slice(P // 16 * first, P // 16 * (first + count))
             picked = work.tile([P, 2, width], F32, name="picked", bufs=8)
-            term = work.tile([P, 2, width], F32, name="term", bufs=8)
+            term = work.tile([P, 2, width], F32, name="term", bufs=3)
             for k in range(2):
                 nc.scalar.activation(picked[:, k, :], y_sb[t][:].indirect(n_sb[k][:, entries]), ACT.Copy)
             nc.vector.tensor_tensor(term[:], picked[:], a_sb[:, :, t, cols], ALU.mult)
@@ -192,20 +194,19 @@ def tile_picked_yskrig_var_p_kernel(
                 for k in range(2):
                     add_transposed(sum_bank[first + bb][:, t, :], term[:, k, part], k == 0, k == 1)
 
-        def second_product(first, count, copy_words, copy_result, word_tag, out_tag):
+        def hidden(b, word_bank):
+            hid = work.tile([P, H], BF16, name="hid", bufs=4)
+            nc.vector.tensor_tensor(
+                hid[:].rearrange("j (t p) -> j t p", p=P), sum_bank[b][:], factor[:, :, P * b : P * (b + 1)], ALU.mult
+            )
+            words = hid[:].bitcast(F32)
+            for u in range(2):
+                nc.tensor.transpose(word_bank[:, u, :], words[:, u : H // 2 : 2], ident[:])
+
+        def second_product(first, count, word_bank, out_tag, copy_result):
             width = P * count
-            word_bank = psum.tile([P, count, 2, P], F32, name="word_bank", tag=word_tag)
-            for bb in range(count):
-                b = first + bb
-                hid = work.tile([P, H], BF16, name="hid", bufs=4)
-                nc.vector.tensor_tensor(
-                    hid[:].rearrange("j (t p) -> j t p", p=P), sum_bank[b][:], factor[:, :, P * b : P * (b + 1)], ALU.mult
-                )
-                words = hid[:].bitcast(F32)
-                for u in range(2):
-                    nc.tensor.transpose(word_bank[:, bb, u, :], words[:, u : H // 2 : 2], ident[:])
             grouped = work.tile([P, width * 4], BF16, name="grouped", align_bytes=64, bufs=3)
-            copy_words(
+            nc.scalar.copy(
                 grouped[:].bitcast(F32).rearrange("p (b j u) -> p b j u", b=count, u=2),
                 word_bank[:].rearrange("p b u j -> p b j u"),
             )
@@ -234,34 +235,47 @@ def tile_picked_yskrig_var_p_kernel(
             squares(t)
         covariances(1)
         nc.scalar.activation(log_dn2[:], dn2[:], ACT.Ln)
+        weights(0)
+        turn_variance(0, "sum0")
         gather_planes()
-        move_plane(nc.gpsimd)
-        gather_words(0)
-        gather_words(1)
+        move_plane(nc.sync)
+        load_scale_rows(nc.sync, w2_plane, w2_scales)
+        nc.sync.dma_start(out=w2_sb[:].bitcast(I32), in_=w2_words[0].bitcast(I32))
+        weights(1)
+        turn_variance(1, "sum1")
+        for o in range(PASSES):
+            gather_words(o)
         y_bank = [psum.tile([P, S], F32, name=f"y_bank{t}", tag=f"wide{t}") for t in range(TILES)]
-        first_product(0)
-        first_product(1)
-        for t in range(2):
-            weights(t)
-            turn_variance(t)
+        for o in range(PASSES):
+            first_product(o)
         covariances(2)
         covariances(3)
-        for t in range(TILES):
-            leave_bank(t)
+        inv_dn2 = keep.tile([P, TILES, S], F32, name="inv_dn2", tag=f"h0_{TILES - 1}")
         for t in range(TILES):
             inverse(t)
-        sum_bank = [psum.tile([P, TILES, P], F32, name=f"sum_bank{b}", tag=f"wide{b}") for b in range(BLOCKS)]
+        for t in range(TILES):
+            leave_bank(t)
         for t in range(2, TILES):
             weights(t)
-            turn_variance(t)
+            turn_variance(t, f"wide{t - 2}")
         for t in range(TILES - 1):
             variance(t)
+        sum_bank = [psum.tile([P, TILES, P], F32, name=f"sum_bank{b}", tag=f"sum{(b + 2) % BLOCKS}") for b in range(BLOCKS)]
         for t in range(TILES - 1):
             neighbours(0, 2, t)
         variance(TILES - 1)
         neighbours(0, 2, TILES - 1)
-        second_product(0, 2, nc.scalar.copy, nc.scalar.copy, "var0", "var1")
-        for t in range(TILES):
-            neighbours(2, 2, t)
-        second_product(2, 1, nc.scalar.copy, nc.scalar.copy, "var2", "wide0")
-        second_product(3, 1, nc.scalar.copy, nc.vector.tensor_copy, "var3", "wide1")
+        word_banks = [
+            psum.tile([P, count, 2, P], F32, name="word_bank", tag=tag) for count, tag in ((2, "wide2"), (1, "wide3"), (1, "wide0"))
+        ]
+        neighbours(2, 2, 0)
+        hidden(0, word_banks[0][:, 0])
+        neighbours(2, 2, 1)
+        hidden(1, word_banks[0][:, 1])
+        neighbours(2, 2, 2)
+        neighbours(2, 2, 3)
+        hidden(2, word_banks[1][:, 0])
+        hidden(3, word_banks[2][:, 0])
+        second_product(0, 2, word_banks[0], "wide1", nc.scalar.copy)
+        second_product(2, 1, word_banks[1], "sum2", nc.scalar.copy)
+        second_product(3, 1, word_banks[2], "sum3", nc.vector.tensor_copy)

import math
from contextlib import ExitStack

import concourse.mybir as mybir
from concourse.masks import make_identity

K, T, S, N, H = 1024, 2048, 512, 256, 512
FLOPS = 2 * K * H * S + 2 * H * N * S

F32 = mybir.dt.float32
BF16 = mybir.dt.bfloat16
I32 = mybir.dt.int32
U32 = mybir.dt.uint32
U16 = mybir.dt.uint16
U8 = mybir.dt.uint8
FP8X4 = mybir.dt.float8_e4m3fn_x4
FP4X4 = mybir.dt.float4_e2m1fn_x4
ALU = mybir.AluOpType
ACT = mybir.ActivationFunctionType

P = 128
PASSES = K // 512
TILES = H // P
BLOCKS = S // P
HALF = S // 2
PAD = 1.05 / 0.9
ROOT = math.sqrt(0.9)


def tile_picked_yskrig_var_p_kernel(
    tc, x_words, x_scales, w1_words, w1_scales, h1, h2, rho, unit, w2_words, w2_scales, offs, n1, n2, out
):
    nc = tc.nc
    with ExitStack() as ctx:
        keep = ctx.enter_context(tc.tile_pool(name="keep", bufs=1))
        work = ctx.enter_context(tc.tile_pool(name="work", bufs=2))
        psum = ctx.enter_context(tc.psum_pool(name="psum", bufs=1))

        def load_scale_rows(queue, plane, scales):
            for q in range(4):
                queue.dma_start(
                    out=plane[32 * q : 32 * q + 4, :, :].bitcast(I32),
                    in_=scales[:, 4 * q : 4 * q + 4, :].rearrange("o r c -> r o c").bitcast(I32),
                )

        def load_x_plane(queues):
            for q in range(4):
                queues[q].dma_start(
                    out=x_plane[32 * q : 32 * q + 4 * PASSES, :].bitcast(I32),
                    in_=x_scales[:, 4 * q : 4 * q + 4, :].bitcast(I32),
                )

        def add_transposed(bank_cols, term, start, stop):
            nc.tensor.matmul(bank_cols, lhsT=term, rhs=ident[:], start=start, stop=stop, is_transpose=True)

        offs_sb = keep.tile([P, S // 16], U16, name="offs_sb")
        n_sb = [keep.tile([P, S // 16], U16, name=f"n{k}_sb") for k in (1, 2)]
        x_plane = keep.tile([P, T], U8, name="x_plane", align_bytes=64)
        w1_plane = keep.tile([P, PASSES, H], U8, name="w1_plane", align_bytes=64)
        w2_plane = keep.tile([P, 1, N], U8, name="w2_plane", align_bytes=64)
        ident = keep.tile([P, P], F32, name="ident")
        x_sb = [keep.tile([P, T], I32, name=f"x_sb{o}", align_bytes=64) for o in range(PASSES)]
        w1_sb = keep.tile([P, PASSES, 2 * H], U8, name="w1_sb", align_bytes=64)
        w2_sb = keep.tile([P, 2 * N], U8, name="w2_sb", align_bytes=64)
        unit_sb = keep.tile([P, TILES], F32, name="unit_sb")
        rho_sb = keep.tile([P, TILES, S], F32, name="rho_sb")
        h_sb = [[keep.tile([P, S], F32, name=f"h{k}_{t}", tag=f"h{k}_{t}") for k in range(2)] for t in range(TILES)]

        xg_words = [keep.tile([P, S], U32, name=f"xg_words{o}", align_bytes=64) for o in range(PASSES)]
        xg_plane = [keep.tile([P, S], U8, name=f"xg_plane{o}", align_bytes=64) for o in range(PASSES)]
        make_identity(nc, ident[:])
        nc.vector.memset(x_plane[:].bitcast(I32), 0)

        def load_h(k, t, queue=nc.sync):
            queue.dma_start(out=h_sb[t][k][:], in_=(h1, h2)[k][P * t : P * (t + 1), :])

        def load_rho(first, count, queue=nc.sync):
            rows = rho[P * first : P * (first + count), :].rearrange("(t p) j -> p t j", p=P)
            queue.dma_start(out=rho_sb[:, first : first + count, :], in_=rows)

        def load_x(o):
            nc.sync.dma_start(out=x_sb[o][:], in_=x_words[o].rearrange("p c r -> p (c r)").bitcast(I32))

        load_rho(0, 1)
        load_rho(1, 1)
        load_rho(2, 1)
        load_rho(3, 1)
        load_h(0, 0)
        load_h(1, 0)
        load_h(0, 1)
        load_h(1, 1)
        load_x_plane((nc.sync,) * 4)
        nc.sync.dma_start(offs_sb[:], offs)
        load_x(0)
        load_h(0, 2)
        load_h(1, 2)
        load_x(1)
        nc.sync.dma_start(out=w1_sb[:].bitcast(I32), in_=w1_words.rearrange("o p c -> p o c").bitcast(I32))
        load_h(0, 3)
        load_h(1, 3)
        load_scale_rows(nc.sync, w1_plane, w1_scales)
        with nc.allow_non_contiguous_dma(reason="one value a row"):
            nc.sync.dma_start(out=unit_sb[:], in_=unit.rearrange("(t p) o -> p (t o)", p=P))
        nc.sync.dma_start(n_sb[0][:], n1)
        nc.sync.dma_start(n_sb[1][:], n2)


        sq = keep.tile([P, TILES, S], F32, name="sq")
        dn2 = keep.tile([P, TILES, S], F32, name="dn2")
        log_dn2 = keep.tile([P, TILES, S], F32, name="log_dn2")
        cov = keep.tile([P, 2, TILES, S], F32, name="cov")
        a_sb = keep.tile([P, 2, TILES, S], F32, name="a_sb")
        prod = keep.tile([P, 2, TILES, S], F32, name="prod")
        factor = keep.tile([P, TILES, S], F32, name="factor")
        var_bank = {}
        y_sb = [keep.tile([P, S], F32, name=f"y_sb{t}") for t in range(TILES)]

        def covariances(t):
            for k in range(2):
                nc.scalar.activation(cov[:, k, t, :], h_sb[t][k][:], ACT.Exp, scale=-1.0)

        def squares(t):
            nc.vector.tensor_tensor(sq[:, t, :], rho_sb[:, t, :], rho_sb[:, t, :], ALU.mult)
            sq_bank = psum.tile([P, S], F32, name="sq_bank", tag=f"wide{t}")
            for b in range(BLOCKS):
                cols = slice(P * b, P * (b + 1))
                add_transposed(sq_bank[:, cols], sq[:, t, cols], True, True)
            nc.scalar.activation(dn2[:, t, :], sq_bank[:], ACT.Square, bias=1.05 / ROOT, scale=-ROOT)

        def weights(t):
            cross = work.tile([P, 2, S], F32, name="cross")
            for k in (1, 0):
                nc.vector.tensor_tensor(cross[:, k, :], rho_sb[:, t, :], cov[:, 1 - k, t, :], ALU.mult)
            for k in (1, 0):
                nc.vector.tensor_tensor(a_sb[:, k, t, :], cross[:, k, :], cov[:, k, t, :], ALU.subtract)
            for k in (1, 0):
                nc.vector.scalar_tensor_tensor(
                    prod[:, k, t, :], a_sb[:, k, t, :], -1.0, cov[:, k, t, :], ALU.mult, ALU.mult
                )

        def gather_words(o):
            nc.vector.tensor_copy(xg_words[o][:], x_sb[o][:].bitcast(U32).indirect(offs_sb[:]))

        def first_product(o):
            for t in range(TILES):
                nc.tensor.matmul_mx(
                    out=y_bank[t][:],
                    lhsT=w1_sb[:, o, 2 * P * t : 2 * P * (t + 1)].bitcast(FP4X4),
                    lhsT_scale=w1_plane[:, o, P * t : P * (t + 1)],
                    rhs=xg_words[o][:].bitcast(FP8X4),
                    rhs_scale=xg_plane[o][:],
                    start=(o == 0),
                    stop=(o == PASSES - 1),
                )

        def leave_bank(t):
            nc.scalar.activation(y_sb[t][:], y_bank[t][:], ACT.Copy, scale=unit_sb[:, t : t + 1])

        def gather_planes():
            nc.vector.tensor_copy(xg_plane[0][:], x_plane[:].indirect(offs_sb[:]))

        def move_plane(queue):
            for q in range(4):
                queue.dma_start(
                    out=xg_plane[1][32 * q : 32 * q + 4, :].bitcast(I32),
                    in_=xg_plane[0][32 * q + 4 : 32 * q + 8, :].bitcast(I32),
                )

        def inverse(t):
            nc.scalar.activation(inv_dn2[:, t, :], log_dn2[:, t, :], ACT.Exp, scale=-1.0)

        def turn_variance(t, tag):
            var_bank[t] = psum.tile([P, S], F32, name="var_bank", tag=tag)
            for b in range(BLOCKS):
                cols = slice(P * b, P * (b + 1))
                terms = (prod[:, 1, t, cols], prod[:, 0, t, cols], sq[:, t, cols])
                for n, term in enumerate(terms):
                    add_transposed(var_bank[t][:, cols], term, n == 0, n == len(terms) - 1)

        def variance(t):
            nc.vector.scalar_tensor_tensor(factor[:, t, :], var_bank[t][:], -PAD, inv_dn2[:, t, :], ALU.add, ALU.mult)

        def neighbours(first, count, t):
            width = P * count
            cols = slice(P * first, P * first + width)
            entries = slice(P // 16 * first, P // 16 * (first + count))
            picked = work.tile([P, 2, width], F32, name="picked", bufs=8)
            term = work.tile([P, 2, width], F32, name="term", bufs=3)
            for k in range(2):
                nc.scalar.activation(picked[:, k, :], y_sb[t][:].indirect(n_sb[k][:, entries]), ACT.Copy)
            nc.vector.tensor_tensor(term[:], picked[:], a_sb[:, :, t, cols], ALU.mult)
            for bb in range(count):
                part = slice(P * bb, P * (bb + 1))
                for k in range(2):
                    add_transposed(sum_bank[first + bb][:, t, :], term[:, k, part], k == 0, k == 1)

        def hidden(b, word_bank):
            hid = work.tile([P, H], BF16, name="hid", bufs=4)
            nc.vector.tensor_tensor(
                hid[:].rearrange("j (t p) -> j t p", p=P), sum_bank[b][:], factor[:, :, P * b : P * (b + 1)], ALU.mult
            )
            words = hid[:].bitcast(F32)
            for u in range(2):
                nc.tensor.transpose(word_bank[:, u, :], words[:, u : H // 2 : 2], ident[:])

        def second_product(first, count, word_bank, out_tag, copy_result):
            width = P * count
            grouped = work.tile([P, width * 4], BF16, name="grouped", align_bytes=64, bufs=3)
            nc.scalar.copy(
                grouped[:].bitcast(F32).rearrange("p (b j u) -> p b j u", b=count, u=2),
                word_bank[:].rearrange("p b u j -> p b j u"),
            )
            codes = work.tile([P, width], U32, name="codes", align_bytes=64, bufs=3)
            plane = work.tile([P, width], U8, name="plane", align_bytes=64, bufs=3)
            nc.vector.quantize_mx(out=codes[:].bitcast(FP8X4), scales=plane[:], in_=grouped[:])
            out_bank = psum.tile([P, 2, width], F32, name="out_bank", tag=out_tag)
            for m in range(2):
                nc.tensor.matmul_mx(
                    out=out_bank[:, m, :],
                    lhsT=w2_sb[:, 2 * P * m : 2 * P * (m + 1)].bitcast(FP4X4),
                    lhsT_scale=w2_plane[:, 0, P * m : P * (m + 1)],
                    rhs=codes[:].bitcast(FP8X4),
                    rhs_scale=plane[:],
                    start=True,
                    stop=True,
                )
            result = work.tile([P, 2, width], F32, name="result", bufs=3)
            copy_result(result[:], out_bank[:])
            nc.sync.dma_start(
                out=out.rearrange("(m p) j -> p m j", p=P)[:, :, P * first : P * first + width], in_=result[:]
            )

        covariances(0)
        for t in range(TILES):
            squares(t)
        covariances(1)
        nc.scalar.activation(log_dn2[:], dn2[:], ACT.Ln)
        weights(0)
        turn_variance(0, "sum0")
        gather_planes()
        move_plane(nc.sync)
        load_scale_rows(nc.sync, w2_plane, w2_scales)
        nc.sync.dma_start(out=w2_sb[:].bitcast(I32), in_=w2_words[0].bitcast(I32))
        weights(1)
        turn_variance(1, "sum1")
        for o in range(PASSES):
            gather_words(o)
        y_bank = [psum.tile([P, S], F32, name=f"y_bank{t}", tag=f"wide{t}") for t in range(TILES)]
        for o in range(PASSES):
            first_product(o)
        covariances(2)
        covariances(3)
        inv_dn2 = keep.tile([P, TILES, S], F32, name="inv_dn2", tag=f"h0_{TILES - 1}")
        for t in range(TILES):
            inverse(t)
        for t in range(TILES):
            leave_bank(t)
        for t in range(2, TILES):
            weights(t)
            turn_variance(t, f"wide{t - 2}")
        for t in range(TILES - 1):
            variance(t)
        sum_bank = [psum.tile([P, TILES, P], F32, name=f"sum_bank{b}", tag=f"sum{(b + 2) % BLOCKS}") for b in range(BLOCKS)]
        for t in range(TILES - 1):
            neighbours(0, 2, t)
        variance(TILES - 1)
        neighbours(0, 2, TILES - 1)
        word_banks = [
            psum.tile([P, count, 2, P], F32, name="word_bank", tag=tag) for count, tag in ((2, "wide2"), (1, "wide3"), (1, "wide0"))
        ]
        neighbours(2, 2, 0)
        hidden(0, word_banks[0][:, 0])
        neighbours(2, 2, 1)
        hidden(1, word_banks[0][:, 1])
        neighbours(2, 2, 2)
        neighbours(2, 2, 3)
        hidden(2, word_banks[1][:, 0])
        hidden(3, word_banks[2][:, 0])
        second_product(0, 2, word_banks[0], "wide1", nc.scalar.copy)
        second_product(2, 1, word_banks[1], "sum2", nc.scalar.copy)
        second_product(3, 1, word_banks[2], "sum3", nc.vector.tensor_copy)
